import numpy as np
import ml_dtypes


def mxq(x, axis, fmt="e4m3"):
    dtype, down = {"e4m3": (ml_dtypes.float8_e4m3fn, 7), "e5m2": (ml_dtypes.float8_e5m2, 14)}[fmt]
    v = np.moveaxis(np.asarray(x, np.float32).astype(ml_dtypes.bfloat16).astype(np.float64), axis, -1)
    blocks = v.reshape(v.shape[:-1] + (-1, 32))
    amax = np.abs(blocks).max(-1, keepdims=True)
    byte = np.maximum(np.where(amax > 0, np.frexp(amax)[1] - 1 + 127, 0) - down, 1)
    scale = np.exp2(byte - 127.0)
    codes = (blocks / scale).astype(np.float32).astype(dtype).astype(np.float64)
    return np.moveaxis((codes * scale).reshape(v.shape), -1, axis)


WIDE = False


def mx_kscale(k):
    if not WIDE:
        return np.ones(k)
    levels = np.array([24, -24, 12, -12, 0])
    if k % 512:
        return np.exp2(np.random.permutation(np.resize(levels, k // 32))).repeat(32)
    a = np.empty((k // 512, 16))
    for p in range(k // 512):
        a[p, :8] = np.random.permutation(np.resize(levels, 8))
        for g in range(8):
            far = levels[np.abs(levels - a[p, g]) >= 10]
            a[p, g + 8] = far[np.random.randint(len(far))]
    return np.exp2(a.ravel()).repeat(32)


def f64(x):
    return np.asarray(x).astype(np.float64)


E2M1 = np.array([0.0, 0.5, 1.0, 1.5, 2.0, 3.0, 4.0, 6.0, -0.0, -0.5, -1.0, -1.5, -2.0, -3.0, -4.0, -6.0])


def pack_weight(w, fmt):
    k, n = w.shape
    w = f64(np.asarray(w, np.float32).astype(ml_dtypes.bfloat16)).reshape(k // 32, 32, n)
    amax = np.abs(w).max(1)
    if fmt == "e4m3":
        byte = np.frexp(amax)[1] - 1 + 127 - 7
    else:
        mant, ex = np.frexp(amax / 6.0)
        byte = np.where(mant > 0.5, ex, ex - 1) + 127
    byte = np.clip(np.where(amax > 0, byte, 1), 1, 254)
    scaled = (w * np.exp2(127.0 - byte)[:, None, :]).reshape(k, n).astype(np.float32)
    by_word = np.ascontiguousarray(scaled.reshape(k // 512, 128, 4, n).transpose(0, 1, 3, 2))
    if fmt == "e4m3":
        words = by_word.astype(ml_dtypes.float8_e4m3fn).view(np.uint8)
    else:
        c = by_word.astype(ml_dtypes.float4_e2m1fn).view(np.uint8) & 0xF
        words = (c[..., 0::2] | (c[..., 1::2] << 4)).reshape(k // 512, 128, 2 * n)
    return np.ascontiguousarray(words), np.ascontiguousarray(byte.astype(np.uint8).reshape(k // 512, 16, n))


def unpack_weight(words, scales, fmt):
    g, _, n = scales.shape
    words = np.ascontiguousarray(words).reshape(g, 128, n, -1)
    if fmt == "e4m3":
        vals = words.view(ml_dtypes.float8_e4m3fn).astype(np.float64)
    else:
        nib = np.empty((g, 128, n, 4), np.uint8)
        nib[..., 0::2] = words & 0xF
        nib[..., 1::2] = words >> 4
        vals = E2M1[nib]
    vals = vals * np.repeat(np.exp2(scales.astype(np.float64) - 127.0), 8, axis=1)[..., None]
    return vals.transpose(0, 1, 3, 2).reshape(g * 512, n)


def silu(f):
    return f / (1.0 + np.exp(-np.maximum(f, -700.0)))


K, F, T = 1024, 512, 1024


def setup_inputs():
    n = np.random.standard_normal
    s = mx_kscale(K)[:, None]
    v = n((K, F)) / np.sqrt(K)
    p_v8 = pack_weight(v / s, "e4m3")
    p_vs = pack_weight(v ** 2 / s ** 2, "e2m1")
    return {
        "x": (n((K, T)) * s).astype(np.float32),
        "v8_words": p_v8[0],
        "v8_scales": p_v8[1],
        "vs_words": p_vs[0],
        "vs_scales": p_vs[1],
        "b": (0.3 * n(F)).astype(np.float32),
    }


def reference(x, v8_words, v8_scales, vs_words, vs_scales, b):
    x_ = mxq(f64(x), 0, "e4m3")
    xs_ = mxq(f64(x) * f64(x), 0, "e4m3")
    v8_ = unpack_weight(v8_words, v8_scales, "e4m3")
    vs_ = unpack_weight(vs_words, vs_scales, "e2m1")
    a = v8_.T @ x_
    c = vs_.T @ xs_
    return silu(0.5 * (a * a - c) + f64(b)[:, None])

@@ -1,0 +1,250 @@
+from contextlib import ExitStack
+
+import concourse.mybir as mybir
+from concourse.masks import make_identity
+
+K, F, T = 1024, 512, 1024
+FLOPS = 2 * 2 * K * F * T
+
+F32 = mybir.dt.float32
+BF16 = mybir.dt.bfloat16
+I32 = mybir.dt.int32
+U32 = mybir.dt.uint32
+U8 = mybir.dt.uint8
+FP8X4 = mybir.dt.float8_e4m3fn_x4
+FP4X4 = mybir.dt.float4_e2m1fn_x4
+ACT = mybir.ActivationFunctionType
+ALU = mybir.AluOpType
+
+P = 128
+PACK = 4
+K_PASS = P * PACK
+PASSES = K // K_PASS
+F_TILES = F // P
+BANK = 512
+RUN = 4
+N_FP4 = 128
+WIDTHS = (256, 256, 256, 128, 128)
+FIRST_PIECES = 1
+NOW = 1
+S8Q = "scalar"
+GROUPS = (2, 2, 2, 1, 2)
+VECTOR_COLS = ((0, 0), (64, 0), (128, 0), (64, 0), (64, 0))
+LOADS = "x00 s8 b x01 w80 ws0 ss x10 w81 ws1 x11"
+
+
+def tile_mix_fm_silu_kernel(tc, x, v8_words, v8_scales, vs_words, vs_scales, b, out):
+    nc = tc.nc
+    starts = [sum(WIDTHS[:c]) for c in range(len(WIDTHS))]
+    chunks = range(len(WIDTHS))
+
+    with ExitStack() as ctx:
+        keep = ctx.enter_context(tc.tile_pool(name="keep", bufs=1))
+        psum = ctx.enter_context(tc.psum_pool(name="psum", bufs=4))
+        ctx.enter_context(tc.manual_schedule())
+
+        v8_w = [keep.tile([P, PASSES, 2 * F], U8, name="v8_w%d" % h, align_bytes=64) for h in range(2)]
+        vs_w = [keep.tile([P, PASSES, F], U8, name="vs_w%d" % h, align_bytes=64) for h in range(2)]
+        v8_s = keep.tile([P, PASSES, F], U8, align_bytes=64)
+        vs_s = keep.tile([P, PASSES, F], U8, align_bytes=64)
+        bias = keep.tile([P, F_TILES], F32)
+        warm = keep.tile([P, 2], F32)
+        bias_rows = keep.tile([P, P], F32)
+        ident = keep.tile([P, P], F32)
+
+        raw, rounded, codes, planes, banks, squares, diffs = {}, {}, {}, {}, {}, {}, {}
+
+        def pieces(c, g):
+            n = FIRST_PIECES if (c, g) == (0, 0) else 1
+            return [(i * WIDTHS[c] // n, WIDTHS[c] // n) for i in range(n)]
+
+        def load_x(c, g):
+            for t0, width in pieces(c, g):
+                raw[c, g, t0] = keep.tile([P, PACK, width], F32, name="raw%d_%d_%d" % (c, g, t0))
+                rows = x[g * K_PASS : (g + 1) * K_PASS, starts[c] + t0 : starts[c] + t0 + width]
+                nc.sync.dma_start(out=raw[c, g, t0][:], in_=rows.rearrange("(p j) w -> p j w", j=PACK))
+
+        def load_scales(queue, plane, scales):
+            for q in range(4):
+                rows = scales[:, 4 * q : 4 * q + 4, :].rearrange("a r f -> r a f")
+                queue.dma_start(out=plane[32 * q : 32 * q + 4, :, :].bitcast(I32), in_=rows.bitcast(I32))
+
+        def views(c, g, which):
+            rounded[c, g, which] = keep.tile(
+                [P, WIDTHS[c] * PACK], BF16, name="%s%d_%d" % (which, c, g), align_bytes=64
+            )
+            pairs = []
+            for t0, width in pieces(c, g):
+                dst = rounded[c, g, which][:, t0 * PACK : (t0 + width) * PACK]
+                pairs.append(
+                    (
+                        dst.rearrange("p (u i j) -> p u j i", i=RUN, j=PACK),
+                        raw[c, g, t0][:].rearrange("p j (u i) -> p u j i", i=RUN),
+                    )
+                )
+            return pairs
+
+        def round_x(c, g):
+            for dst, src in views(c, g, "x"):
+                nc.vector.tensor_copy(out=dst, in_=src)
+
+        def square_x(c, g):
+            cut = VECTOR_COLS[c][g] // RUN
+            for dst, src in views(c, g, "xs"):
+                if cut > 0:
+                    nc.vector.tensor_tensor(out=dst[:, :cut], in0=src[:, :cut], in1=src[:, :cut], op=ALU.mult)
+                if cut < dst.shape[1]:
+                    nc.scalar.activation(out=dst[:, cut:], in_=src[:, cut:], func=ACT.Square)
+
+        def quantize(c, g, which):
+            key = (c, g, which)
+            codes[key] = keep.tile([P, WIDTHS[c]], U32, name="codes_%s%d_%d" % (which, c, g), align_bytes=64)
+            planes[key] = keep.tile([P, WIDTHS[c]], U8, name="plane_%s%d_%d" % (which, c, g), align_bytes=64)
+            nc.vector.quantize_mx(out=codes[key][:].bitcast(FP8X4), scales=planes[key][:], in_=rounded[key][:])
+
+        def tiles_of(c, h):
+            per_bank = F_TILES // GROUPS[c]
+            return range(h * per_bank, (h + 1) * per_bank)
+
+        def halves(c):
+            return range(GROUPS[c])
+
+        def span(c):
+            return F_TILES // GROUPS[c] * WIDTHS[c]
+
+        def multiply(c, g, which, groups):
+            key = (c, g, which)
+            width = WIDTHS[c]
+            n = width if which == "x" else N_FP4
+            for h in groups:
+                if g == 0:
+                    banks[c, h, which] = psum.tile([P, BANK], F32, name="acc_" + which)
+                steps = [(m, t0) for m in tiles_of(c, h) for t0 in range(0, width, n)]
+                for s, (m, t0) in enumerate(steps):
+                    if which == "x":
+                        lhsT = v8_w[m // 2][:, g, 4 * P * (m % 2) : 4 * P * (m % 2 + 1)].bitcast(FP8X4)
+                        lhsT_scale = v8_s[:, g, P * m : P * (m + 1)]
+                    else:
+                        lhsT = vs_w[m // 2][:, g, 2 * P * (m % 2) : 2 * P * (m % 2 + 1)].bitcast(FP4X4)
+                        lhsT_scale = vs_s[:, g, P * m : P * (m + 1)]
+                    nc.tensor.matmul_mx(
+                        out=banks[c, h, which][:, s * n : (s + 1) * n],
+                        lhsT=lhsT,
+                        lhsT_scale=lhsT_scale,
+                        rhs=codes[key][:, t0 : t0 + n].bitcast(FP8X4),
+                        rhs_scale=planes[key][:, t0 : t0 + n],
+                        start=(g == 0 and s == 0),
+                        stop=(g == PASSES - 1 and s == len(steps) - 1),
+                    )
+
+        def square_a(c, h):
+            squares[c, h] = keep.tile([P, span(c)], F32, name="asq%d_%d" % (c, h))
+            nc.scalar.activation(out=squares[c, h][:], in_=banks[c, h, "x"][:, : span(c)], func=ACT.Square)
+
+        def subtract(c, h):
+            diffs[c, h] = keep.tile([P, span(c)], F32, name="diff%d_%d" % (c, h))
+            nc.vector.tensor_tensor(
+                out=diffs[c, h][:], in0=squares[c, h][:], in1=banks[c, h, "xs"][:, : span(c)], op=ALU.subtract
+            )
+
+        def finish(c, h):
+            width = WIDTHS[c]
+            tiles = tiles_of(c, h)
+            result = keep.tile([P, len(tiles), width], F32, name="res%d_%d" % (c, h))
+            for s, m in enumerate(tiles):
+                nc.scalar.activation(
+                    out=result[:, s, :],
+                    in_=diffs[c, h][:, s * width : (s + 1) * width],
+                    func=ACT.Silu,
+                    bias=bias[:, m : m + 1],
+                    scale=0.5,
+                )
+            rows = out[tiles[0] * P : (tiles[-1] + 1) * P, starts[c] : starts[c] + width]
+            nc.sync.dma_start(out=rows.rearrange("(m p) w -> p m w", p=P), in_=result[:])
+
+        nc.vector.memset(v8_s[:].bitcast(U32), 0)
+        nc.vector.memset(warm[:], 0.0)
+        nc.vector.memset(vs_s[:].bitcast(U32), 0)
+        nc.gpsimd.memset(bias_rows[:], 0.0)
+        make_identity(nc, ident[:])
+
+        v8_rows = v8_words.rearrange("a p f i -> p a (f i)").bitcast(I32)
+        vs_rows = vs_words.rearrange("a p n -> p a n").bitcast(I32)
+        done = []
+        for item in LOADS.split():
+            if item[0] == "x":
+                load_x(int(item[1]), int(item[2]))
+                done.append((int(item[1]), int(item[2])))
+            elif item == "s8":
+                load_scales(nc.scalar if S8Q == "scalar" else nc.sync, v8_s, v8_scales)
+            elif item == "ss":
+                load_scales(nc.sync, vs_s, vs_scales)
+            elif item[:2] == "w8":
+                h = int(item[2])
+                nc.sync.dma_start(out=v8_w[h][:].bitcast(I32), in_=v8_rows[:, :, h * F // 2 : (h + 1) * F // 2])
+            elif item[:2] == "ws":
+                h = int(item[2])
+                nc.sync.dma_start(out=vs_w[h][:].bitcast(I32), in_=vs_rows[:, :, h * F // 4 : (h + 1) * F // 4])
+            else:
+                nc.gpsimd.dma_start(out=bias_rows[:F_TILES, :], in_=b.rearrange("(m p) -> m p", p=P))
+        for c in chunks:
+            for g in range(PASSES):
+                if (c, g) not in done:
+                    load_x(c, g)
+
+        nc.scalar.activation(out=warm[:, 1:2], in_=warm[:, 0:1], func=ACT.Silu)
+
+        bias_t = psum.tile([P, BANK], F32, name="acc_xs")
+        nc.tensor.transpose(bias_t[:, :P], bias_rows[:], ident[:])
+        round_x(0, 0)
+        square_x(0, 0)
+        quantize(0, 0, "x")
+        round_x(0, 1)
+        square_x(0, 1)
+        quantize(0, 0, "xs")
+        quantize(0, 1, "x")
+        quantize(0, 1, "xs")
+        nc.vector.tensor_copy(out=bias[:], in_=bias_t[:, :F_TILES])
+        for h in halves(0):
+            for which in ("x", "xs"):
+                for g in range(PASSES):
+                    multiply(0, g, which, [h])
+        pending = []
+        square_a(0, 0)
+        for c in chunks[1:]:
+            before = halves(c - 1)
+            late = before[1:] if c == 1 else before
+            round_x(c, 0)
+            if c == 1:
+                subtract(0, 0)
+                pending = [(0, 0)]
+            square_x(c, 0)
+            quantize(c, 0, "x")
+            multiply(c, 0, "x", halves(c))
+            for key in pending:
+                finish(*key)
+            for h in late:
+                square_a(c - 1, h)
+            round_x(c, 1)
+            square_x(c, 1)
+            quantize(c, 0, "xs")
+            multiply(c, 0, "xs", halves(c))
+            for h in late[:1]:
+                subtract(c - 1, h)
+            quantize(c, 1, "x")
+            multiply(c, 1, "x", halves(c))
+            for h in late[1:]:
+                subtract(c - 1, h)
+            quantize(c, 1, "xs")
+            multiply(c, 1, "xs", halves(c))
+            for h in late[:NOW]:
+                finish(c - 1, h)
+            pending = [(c - 1, h) for h in late[NOW:]]
+        last = chunks[-1]
+        for key in pending:
+            finish(*key)
+        for h in halves(last):
+            square_a(last, h)
+        for h in halves(last):
+            subtract(last, h)
+            finish(last, h)

@@ -1,7 +1,6 @@
 from contextlib import ExitStack
 
 import concourse.mybir as mybir
-from concourse.masks import make_identity
 
 K, F, T = 1024, 512, 1024
 FLOPS = 2 * 2 * K * F * T
@@ -26,11 +25,13 @@ RUN = 4
 N_FP4 = 128
 WIDTHS = (256, 256, 256, 128, 128)
 FIRST_PIECES = 1
-NOW = 1
+LASTQ = 1
+WARM = 0
+NOW = 0
 S8Q = "scalar"
-GROUPS = (2, 2, 2, 1, 2)
+GROUPS = (2, 2, 2, 2, 2)
 VECTOR_COLS = ((0, 0), (64, 0), (128, 0), (64, 0), (64, 0))
-LOADS = "x00 s8 b x01 w80 ws0 ss x10 w81 ws1 x11"
+LOADS = "x00 s8 x01 w80 ws0 ss x10 w81 ws1 b x11"
 
 
 def tile_mix_fm_silu_kernel(tc, x, v8_words, v8_scales, vs_words, vs_scales, b, out):
@@ -47,10 +48,9 @@ def tile_mix_fm_silu_kernel(tc, x, v8_words, v8_scales, vs_words, vs_scales, b, 
         vs_w = [keep.tile([P, PASSES, F], U8, name="vs_w%d" % h, align_bytes=64) for h in range(2)]
         v8_s = keep.tile([P, PASSES, F], U8, align_bytes=64)
         vs_s = keep.tile([P, PASSES, F], U8, align_bytes=64)
-        bias = keep.tile([P, F_TILES], F32)
+        bias = keep.tile([P, 32], F32, align_bytes=64)
         warm = keep.tile([P, 2], F32)
-        bias_rows = keep.tile([P, P], F32)
-        ident = keep.tile([P, P], F32)
+        bias_rows = keep.tile([P, 32], F32, align_bytes=64)
 
         raw, rounded, codes, planes, banks, squares, diffs = {}, {}, {}, {}, {}, {}, {}
 
@@ -160,13 +160,13 @@ def tile_mix_fm_silu_kernel(tc, x, v8_words, v8_scales, vs_words, vs_scales, b, 
                     scale=0.5,
                 )
             rows = out[tiles[0] * P : (tiles[-1] + 1) * P, starts[c] : starts[c] + width]
-            nc.sync.dma_start(out=rows.rearrange("(m p) w -> p m w", p=P), in_=result[:])
+            queue = nc.scalar if LASTQ and (c, h) == (chunks[-1], halves(c)[-1]) else nc.sync
+            queue.dma_start(out=rows.rearrange("(m p) w -> p m w", p=P), in_=result[:])
 
         nc.vector.memset(v8_s[:].bitcast(U32), 0)
         nc.vector.memset(warm[:], 0.0)
         nc.vector.memset(vs_s[:].bitcast(U32), 0)
-        nc.gpsimd.memset(bias_rows[:], 0.0)
-        make_identity(nc, ident[:])
+        nc.vector.memset(bias_rows[:], 0.0)
 
         v8_rows = v8_words.rearrange("a p f i -> p a (f i)").bitcast(I32)
         vs_rows = vs_words.rearrange("a p n -> p a n").bitcast(I32)
@@ -186,7 +186,9 @@ def tile_mix_fm_silu_kernel(tc, x, v8_words, v8_scales, vs_words, vs_scales, b, 
                 h = int(item[2])
                 nc.sync.dma_start(out=vs_w[h][:].bitcast(I32), in_=vs_rows[:, :, h * F // 4 : (h + 1) * F // 4])
             else:
-                nc.gpsimd.dma_start(out=bias_rows[:F_TILES, :], in_=b.rearrange("(m p) -> m p", p=P))
+                for q in range(4):
+                    rows = b.rearrange("(m q j) -> q m j", q=4, j=32)[q]
+                    nc.sync.dma_start(out=bias_rows[32 * q : 32 * q + F_TILES, :], in_=rows)
         for c in chunks:
             for g in range(PASSES):
                 if (c, g) not in done:
@@ -194,17 +196,26 @@ def tile_mix_fm_silu_kernel(tc, x, v8_words, v8_scales, vs_words, vs_scales, b, 
 
         nc.scalar.activation(out=warm[:, 1:2], in_=warm[:, 0:1], func=ACT.Silu)
 
-        bias_t = psum.tile([P, BANK], F32, name="acc_xs")
-        nc.tensor.transpose(bias_t[:, :P], bias_rows[:], ident[:])
         round_x(0, 0)
         square_x(0, 0)
         quantize(0, 0, "x")
+        if WARM:
+            spare = psum.tile([P, BANK], F32, name="acc_xs")
+            for s in range(WARM):
+                nc.tensor.matmul_mx(
+                    out=spare[:, : WIDTHS[0]],
+                    lhsT=codes[0, 0, "x"][:, :P].bitcast(FP8X4),
+                    lhsT_scale=planes[0, 0, "x"][:, :P],
+                    rhs=codes[0, 0, "x"][:].bitcast(FP8X4),
+                    rhs_scale=planes[0, 0, "x"][:],
+                    start=True,
+                    stop=True,
+                )
         round_x(0, 1)
         square_x(0, 1)
         quantize(0, 0, "xs")
         quantize(0, 1, "x")
         quantize(0, 1, "xs")
-        nc.vector.tensor_copy(out=bias[:], in_=bias_t[:, :F_TILES])
         for h in halves(0):
             for which in ("x", "xs"):
                 for g in range(PASSES):
@@ -217,6 +228,7 @@ def tile_mix_fm_silu_kernel(tc, x, v8_words, v8_scales, vs_words, vs_scales, b, 
             round_x(c, 0)
             if c == 1:
                 subtract(0, 0)
+                nc.vector.transpose(out=bias[:], in_=bias_rows[:])
                 pending = [(0, 0)]
             square_x(c, 0)
             quantize(c, 0, "x")

@@ -16,138 +16,140 @@ ACT = mybir.ActivationFunctionType
 ALU = mybir.AluOpType
 
 P = 128
+QUADRANT = 32
+QUADRANTS = P // QUADRANT
 PACK = 4
 K_PASS = P * PACK
 PASSES = K // K_PASS
 F_TILES = F // P
 BANK = 512
+BANKS_PER_SUM = 4
 RUN = 4
 N_FP4 = 128
-WIDTHS = (256, 256, 256, 128, 128)
-FIRST_PIECES = 1
-LASTQ = 1
-WARM = 0
-NOW = 0
-S8Q = "scalar"
-GROUPS = (2, 2, 2, 2, 2)
-VECTOR_COLS = ((0, 0), (64, 0), (128, 0), (64, 0), (64, 0))
-LOADS = "x00 s8 x01 w80 ws0 ss x10 w81 ws1 b x11"
+WIDTHS = (512, 256, 256)
+GROUPS = (4, 2, 4)
+VECTOR_COLUMNS = (0, 64, 64)
+WARM_PASSES = 3
 
 
 def tile_mix_fm_silu_kernel(tc, x, v8_words, v8_scales, vs_words, vs_scales, b, out):
     nc = tc.nc
     starts = [sum(WIDTHS[:c]) for c in range(len(WIDTHS))]
-    chunks = range(len(WIDTHS))
 
     with ExitStack() as ctx:
         keep = ctx.enter_context(tc.tile_pool(name="keep", bufs=1))
-        psum = ctx.enter_context(tc.psum_pool(name="psum", bufs=4))
+        psum = ctx.enter_context(tc.psum_pool(name="psum", bufs=BANKS_PER_SUM))
         ctx.enter_context(tc.manual_schedule())
 
-        v8_w = [keep.tile([P, PASSES, 2 * F], U8, name="v8_w%d" % h, align_bytes=64) for h in range(2)]
-        vs_w = [keep.tile([P, PASSES, F], U8, name="vs_w%d" % h, align_bytes=64) for h in range(2)]
-        v8_s = keep.tile([P, PASSES, F], U8, align_bytes=64)
-        vs_s = keep.tile([P, PASSES, F], U8, align_bytes=64)
-        bias = keep.tile([P, 32], F32, align_bytes=64)
-        warm = keep.tile([P, 2], F32)
-        bias_rows = keep.tile([P, 32], F32, align_bytes=64)
+        v8_w = [keep.tile([P, PASSES, 4 * P], U8, name="v8_w%d" % m, align_bytes=64) for m in range(F_TILES)]
+        vs_w = [keep.tile([P, PASSES, 2 * P], U8, name="vs_w%d" % m, align_bytes=64) for m in range(F_TILES)]
+        v8_plane = keep.tile([P, PASSES, F], U8, align_bytes=64)
+        vs_plane = keep.tile([P, PASSES, F], U8, align_bytes=64)
+        bias = keep.tile([P, QUADRANT], F32, align_bytes=64)
+        table_warm = keep.tile([P, 2], F32)
+        bias_rows = keep.tile([P, QUADRANT], F32, align_bytes=64)
 
-        raw, rounded, codes, planes, banks, squares, diffs = {}, {}, {}, {}, {}, {}, {}
-
-        def pieces(c, g):
-            n = FIRST_PIECES if (c, g) == (0, 0) else 1
-            return [(i * WIDTHS[c] // n, WIDTHS[c] // n) for i in range(n)]
+        raw, rounded, codes, planes, banks, a_squared, diffs = {}, {}, {}, {}, {}, {}, {}
 
         def load_x(c, g):
-            for t0, width in pieces(c, g):
-                raw[c, g, t0] = keep.tile([P, PACK, width], F32, name="raw%d_%d_%d" % (c, g, t0))
-                rows = x[g * K_PASS : (g + 1) * K_PASS, starts[c] + t0 : starts[c] + t0 + width]
-                nc.sync.dma_start(out=raw[c, g, t0][:], in_=rows.rearrange("(p j) w -> p j w", j=PACK))
+            raw[c, g] = keep.tile([P, PACK, WIDTHS[c]], F32, name="raw%d_%d" % (c, g))
+            rows = x[g * K_PASS : (g + 1) * K_PASS, starts[c] : starts[c] + WIDTHS[c]]
+            nc.sync.dma_start(out=raw[c, g][:], in_=rows.rearrange("(p j) w -> p j w", j=PACK))
 
         def load_scales(queue, plane, scales):
-            for q in range(4):
+            for q in range(QUADRANTS):
                 rows = scales[:, 4 * q : 4 * q + 4, :].rearrange("a r f -> r a f")
-                queue.dma_start(out=plane[32 * q : 32 * q + 4, :, :].bitcast(I32), in_=rows.bitcast(I32))
+                live = plane[QUADRANT * q : QUADRANT * q + 4, :, :]
+                queue.dma_start(out=live.bitcast(I32), in_=rows.bitcast(I32))
 
-        def views(c, g, which):
-            rounded[c, g, which] = keep.tile(
-                [P, WIDTHS[c] * PACK], BF16, name="%s%d_%d" % (which, c, g), align_bytes=64
+        def load_weights(m):
+            v8_rows = v8_words.rearrange("a p f i -> p a (f i)").bitcast(I32)
+            vs_rows = vs_words.rearrange("a p n -> p a n").bitcast(I32)
+            nc.sync.dma_start(out=v8_w[m][:].bitcast(I32), in_=v8_rows[:, :, m * P : (m + 1) * P])
+            nc.sync.dma_start(out=vs_w[m][:].bitcast(I32), in_=vs_rows[:, :, m * P // 2 : (m + 1) * P // 2])
+
+        def load_bias():
+            for q in range(QUADRANTS):
+                rows = b.rearrange("(m q i) -> q m i", q=QUADRANTS, i=QUADRANT)[q]
+                nc.sync.dma_start(out=bias_rows[QUADRANT * q : QUADRANT * q + F_TILES, :], in_=rows)
+
+        def interleaving_views(c, g, operand):
+            rounded[c, g, operand] = keep.tile(
+                [P, WIDTHS[c] * PACK], BF16, name="%s%d_%d" % (operand, c, g), align_bytes=64
             )
-            pairs = []
-            for t0, width in pieces(c, g):
-                dst = rounded[c, g, which][:, t0 * PACK : (t0 + width) * PACK]
-                pairs.append(
-                    (
-                        dst.rearrange("p (u i j) -> p u j i", i=RUN, j=PACK),
-                        raw[c, g, t0][:].rearrange("p j (u i) -> p u j i", i=RUN),
-                    )
-                )
-            return pairs
+            dst = rounded[c, g, operand][:].rearrange("p (u i j) -> p u j i", i=RUN, j=PACK)
+            src = raw[c, g][:].rearrange("p j (u i) -> p u j i", i=RUN)
+            return dst, src
 
         def round_x(c, g):
-            for dst, src in views(c, g, "x"):
-                nc.vector.tensor_copy(out=dst, in_=src)
+            dst, src = interleaving_views(c, g, "x")
+            nc.vector.tensor_copy(out=dst, in_=src)
 
         def square_x(c, g):
-            cut = VECTOR_COLS[c][g] // RUN
-            for dst, src in views(c, g, "xs"):
-                if cut > 0:
-                    nc.vector.tensor_tensor(out=dst[:, :cut], in0=src[:, :cut], in1=src[:, :cut], op=ALU.mult)
-                if cut < dst.shape[1]:
-                    nc.scalar.activation(out=dst[:, cut:], in_=src[:, cut:], func=ACT.Square)
+            dst, src = interleaving_views(c, g, "xs")
+            cut = VECTOR_COLUMNS[c] // RUN
+            if cut > 0:
+                nc.vector.tensor_tensor(out=dst[:, :cut], in0=src[:, :cut], in1=src[:, :cut], op=ALU.mult)
+            nc.scalar.activation(out=dst[:, cut:], in_=src[:, cut:], func=ACT.Square)
 
-        def quantize(c, g, which):
-            key = (c, g, which)
-            codes[key] = keep.tile([P, WIDTHS[c]], U32, name="codes_%s%d_%d" % (which, c, g), align_bytes=64)
-            planes[key] = keep.tile([P, WIDTHS[c]], U8, name="plane_%s%d_%d" % (which, c, g), align_bytes=64)
+        def quantize(c, g, operand):
+            key = (c, g, operand)
+            codes[key] = keep.tile([P, WIDTHS[c]], U32, name="codes_%s%d_%d" % (operand, c, g), align_bytes=64)
+            planes[key] = keep.tile([P, WIDTHS[c]], U8, name="plane_%s%d_%d" % (operand, c, g), align_bytes=64)
             nc.vector.quantize_mx(out=codes[key][:].bitcast(FP8X4), scales=planes[key][:], in_=rounded[key][:])
 
         def tiles_of(c, h):
-            per_bank = F_TILES // GROUPS[c]
-            return range(h * per_bank, (h + 1) * per_bank)
-
-        def halves(c):
-            return range(GROUPS[c])
+            per_group = F_TILES // GROUPS[c]
+            return range(h * per_group, (h + 1) * per_group)
 
         def span(c):
             return F_TILES // GROUPS[c] * WIDTHS[c]
 
-        def multiply(c, g, which, groups):
-            key = (c, g, which)
+        def multiply(c, g, operand, groups):
+            key = (c, g, operand)
             width = WIDTHS[c]
-            n = width if which == "x" else N_FP4
+            n = width if (operand == "x" or width == BANK) else N_FP4
             for h in groups:
                 if g == 0:
-                    banks[c, h, which] = psum.tile([P, BANK], F32, name="acc_" + which)
+                    banks[c, h, operand] = psum.tile([P, BANK], F32, name="acc_" + operand)
                 steps = [(m, t0) for m in tiles_of(c, h) for t0 in range(0, width, n)]
                 for s, (m, t0) in enumerate(steps):
-                    if which == "x":
-                        lhsT = v8_w[m // 2][:, g, 4 * P * (m % 2) : 4 * P * (m % 2 + 1)].bitcast(FP8X4)
-                        lhsT_scale = v8_s[:, g, P * m : P * (m + 1)]
+                    if operand == "x":
+                        weights, weight_plane = v8_w[m][:, g, :].bitcast(FP8X4), v8_plane
                     else:
-                        lhsT = vs_w[m // 2][:, g, 2 * P * (m % 2) : 2 * P * (m % 2 + 1)].bitcast(FP4X4)
-                        lhsT_scale = vs_s[:, g, P * m : P * (m + 1)]
+                        weights, weight_plane = vs_w[m][:, g, :].bitcast(FP4X4), vs_plane
                     nc.tensor.matmul_mx(
-                        out=banks[c, h, which][:, s * n : (s + 1) * n],
-                        lhsT=lhsT,
-                        lhsT_scale=lhsT_scale,
+                        out=banks[c, h, operand][:, s * n : (s + 1) * n],
+                        lhsT=weights,
+                        lhsT_scale=weight_plane[:, g, P * m : P * (m + 1)],
                         rhs=codes[key][:, t0 : t0 + n].bitcast(FP8X4),
                         rhs_scale=planes[key][:, t0 : t0 + n],
                         start=(g == 0 and s == 0),
                         stop=(g == PASSES - 1 and s == len(steps) - 1),
                     )
 
+        def multiply_all_passes(c, operand, h):
+            for g in range(PASSES):
+                multiply(c, g, operand, [h])
+
         def square_a(c, h):
-            squares[c, h] = keep.tile([P, span(c)], F32, name="asq%d_%d" % (c, h))
-            nc.scalar.activation(out=squares[c, h][:], in_=banks[c, h, "x"][:, : span(c)], func=ACT.Square)
+            a_squared[c, h] = keep.tile([P, span(c)], F32, name="asq%d_%d" % (c, h))
+            nc.scalar.activation(out=a_squared[c, h][:], in_=banks[c, h, "x"][:, : span(c)], func=ACT.Square)
+
+        def square_a_on_vector(c, h):
+            acc = banks[c, h, "x"][:, : span(c)]
+            a_squared[c, h] = keep.tile([P, span(c)], F32, name="asq%d_%d" % (c, h))
+            a_copy = keep.tile([P, span(c)], F32)
+            nc.vector.tensor_copy(out=a_copy[:], in_=acc)
+            nc.vector.tensor_tensor(out=a_squared[c, h][:], in0=a_copy[:], in1=acc, op=ALU.mult)
 
         def subtract(c, h):
             diffs[c, h] = keep.tile([P, span(c)], F32, name="diff%d_%d" % (c, h))
             nc.vector.tensor_tensor(
-                out=diffs[c, h][:], in0=squares[c, h][:], in1=banks[c, h, "xs"][:, : span(c)], op=ALU.subtract
+                out=diffs[c, h][:], in0=a_squared[c, h][:], in1=banks[c, h, "xs"][:, : span(c)], op=ALU.subtract
             )
 
-        def finish(c, h):
+        def finish(c, h, queue):
             width = WIDTHS[c]
             tiles = tiles_of(c, h)
             result = keep.tile([P, len(tiles), width], F32, name="res%d_%d" % (c, h))
@@ -160,103 +162,107 @@ def tile_mix_fm_silu_kernel(tc, x, v8_words, v8_scales, vs_words, vs_scales, b, 
                     scale=0.5,
                 )
             rows = out[tiles[0] * P : (tiles[-1] + 1) * P, starts[c] : starts[c] + width]
-            queue = nc.scalar if LASTQ and (c, h) == (chunks[-1], halves(c)[-1]) else nc.sync
             queue.dma_start(out=rows.rearrange("(m p) w -> p m w", p=P), in_=result[:])
 
-        nc.vector.memset(v8_s[:].bitcast(U32), 0)
-        nc.vector.memset(warm[:], 0.0)
-        nc.vector.memset(vs_s[:].bitcast(U32), 0)
+        nc.vector.memset(v8_plane[:].bitcast(U32), 0)
+        nc.vector.memset(table_warm[:], 0.0)
+        nc.vector.memset(vs_plane[:].bitcast(U32), 0)
         nc.vector.memset(bias_rows[:], 0.0)
 
-        v8_rows = v8_words.rearrange("a p f i -> p a (f i)").bitcast(I32)
-        vs_rows = vs_words.rearrange("a p n -> p a n").bitcast(I32)
-        done = []
-        for item in LOADS.split():
-            if item[0] == "x":
-                load_x(int(item[1]), int(item[2]))
-                done.append((int(item[1]), int(item[2])))
-            elif item == "s8":
-                load_scales(nc.scalar if S8Q == "scalar" else nc.sync, v8_s, v8_scales)
-            elif item == "ss":
-                load_scales(nc.sync, vs_s, vs_scales)
-            elif item[:2] == "w8":
-                h = int(item[2])
-                nc.sync.dma_start(out=v8_w[h][:].bitcast(I32), in_=v8_rows[:, :, h * F // 2 : (h + 1) * F // 2])
-            elif item[:2] == "ws":
-                h = int(item[2])
-                nc.sync.dma_start(out=vs_w[h][:].bitcast(I32), in_=vs_rows[:, :, h * F // 4 : (h + 1) * F // 4])
-            else:
-                for q in range(4):
-                    rows = b.rearrange("(m q j) -> q m j", q=4, j=32)[q]
-                    nc.sync.dma_start(out=bias_rows[32 * q : 32 * q + F_TILES, :], in_=rows)
-        for c in chunks:
-            for g in range(PASSES):
-                if (c, g) not in done:
-                    load_x(c, g)
+        load_x(0, 0)
+        load_scales(nc.scalar, v8_plane, v8_scales)
+        load_scales(nc.gpsimd, vs_plane, vs_scales)
+        load_x(0, 1)
+        load_weights(0)
+        load_x(1, 0)
+        load_bias()
+        load_weights(1)
+        load_x(1, 1)
+        load_weights(2)
+        load_weights(3)
+        load_x(2, 0)
+        load_x(2, 1)
 
-        nc.scalar.activation(out=warm[:, 1:2], in_=warm[:, 0:1], func=ACT.Silu)
+        nc.scalar.activation(out=table_warm[:, 1:2], in_=table_warm[:, 0:1], func=ACT.Silu)
 
         round_x(0, 0)
         square_x(0, 0)
         quantize(0, 0, "x")
-        if WARM:
-            spare = psum.tile([P, BANK], F32, name="acc_xs")
-            for s in range(WARM):
-                nc.tensor.matmul_mx(
-                    out=spare[:, : WIDTHS[0]],
-                    lhsT=codes[0, 0, "x"][:, :P].bitcast(FP8X4),
-                    lhsT_scale=planes[0, 0, "x"][:, :P],
-                    rhs=codes[0, 0, "x"][:].bitcast(FP8X4),
-                    rhs_scale=planes[0, 0, "x"][:],
-                    start=True,
-                    stop=True,
-                )
+        warm_bank = psum.tile([P, BANK], F32, name="acc_xs")
+        for n in range(WARM_PASSES):
+            nc.tensor.matmul_mx(
+                out=warm_bank[:],
+                lhsT=codes[0, 0, "x"][:, :P].bitcast(FP8X4),
+                lhsT_scale=planes[0, 0, "x"][:, :P],
+                rhs=codes[0, 0, "x"][:].bitcast(FP8X4),
+                rhs_scale=planes[0, 0, "x"][:],
+                start=True,
+                stop=True,
+            )
         round_x(0, 1)
         square_x(0, 1)
         quantize(0, 0, "xs")
         quantize(0, 1, "x")
         quantize(0, 1, "xs")
-        for h in halves(0):
-            for which in ("x", "xs"):
-                for g in range(PASSES):
-                    multiply(0, g, which, [h])
-        pending = []
+        for h in range(GROUPS[0]):
+            multiply_all_passes(0, "x", h)
+            multiply_all_passes(0, "xs", h)
+
+        round_x(1, 0)
+        square_x(1, 0)
         square_a(0, 0)
-        for c in chunks[1:]:
-            before = halves(c - 1)
-            late = before[1:] if c == 1 else before
-            round_x(c, 0)
-            if c == 1:
-                subtract(0, 0)
-                nc.vector.transpose(out=bias[:], in_=bias_rows[:])
-                pending = [(0, 0)]
-            square_x(c, 0)
-            quantize(c, 0, "x")
-            multiply(c, 0, "x", halves(c))
-            for key in pending:
-                finish(*key)
-            for h in late:
-                square_a(c - 1, h)
-            round_x(c, 1)
-            square_x(c, 1)
-            quantize(c, 0, "xs")
-            multiply(c, 0, "xs", halves(c))
-            for h in late[:1]:
-                subtract(c - 1, h)
-            quantize(c, 1, "x")
-            multiply(c, 1, "x", halves(c))
-            for h in late[1:]:
-                subtract(c - 1, h)
-            quantize(c, 1, "xs")
-            multiply(c, 1, "xs", halves(c))
-            for h in late[:NOW]:
-                finish(c - 1, h)
-            pending = [(c - 1, h) for h in late[NOW:]]
-        last = chunks[-1]
-        for key in pending:
-            finish(*key)
-        for h in halves(last):
-            square_a(last, h)
-        for h in halves(last):
-            subtract(last, h)
-            finish(last, h)
+        quantize(1, 0, "x")
+        subtract(0, 0)
+        square_a(0, 1)
+        nc.vector.transpose(out=bias[:], in_=bias_rows[:])
+
+        round_x(1, 1)
+        square_x(1, 1)
+        finish(0, 0, nc.sync)
+        quantize(1, 0, "xs")
+        subtract(0, 1)
+        square_a(0, 2)
+        quantize(1, 1, "x")
+        quantize(1, 1, "xs")
+        finish(0, 1, nc.sync)
+        for operand in ("x", "xs"):
+            for h in range(GROUPS[1]):
+                multiply_all_passes(1, operand, h)
+        subtract(0, 2)
+        square_a(0, 3)
+
+        round_x(2, 0)
+        square_x(2, 0)
+        finish(0, 2, nc.sync)
+        quantize(2, 0, "x")
+        multiply(2, 0, "x", [0, 1])
+        subtract(0, 3)
+
+        round_x(2, 1)
+        square_a(1, 0)
+        square_x(2, 1)
+        square_a(1, 1)
+        quantize(2, 0, "xs")
+        multiply(2, 0, "xs", [0, 1])
+        quantize(2, 1, "x")
+        multiply(2, 0, "x", [2, 3])
+        multiply(2, 1, "x", [0, 1])
+        finish(0, 3, nc.sync)
+        subtract(1, 0)
+        multiply(2, 0, "xs", [2])
+        multiply(2, 1, "x", [2, 3])
+        quantize(2, 1, "xs")
+        multiply(2, 1, "xs", [0, 1, 2])
+        subtract(1, 1)
+        multiply_all_passes(2, "xs", 3)
+
+        last = GROUPS[2] - 1
+        finish(1, 0, nc.sync)
+        square_a(2, 0)
+        finish(1, 1, nc.sync)
+        for h in range(1, last):
+            square_a(2, h)
+        square_a_on_vector(2, last)
+        for h in range(GROUPS[2]):
+            subtract(2, h)
+            finish(2, h, nc.scalar if h == last else nc.sync)

@@ -29,7 +29,7 @@ N_FP4 = 128
 WIDTHS = (512, 256, 256)
 GROUPS = (4, 2, 4)
 VECTOR_COLUMNS = (0, 64, 64)
-WARM_PASSES = 3
+TILES_PER_LOAD = 2
 
 
 def tile_mix_fm_silu_kernel(tc, x, v8_words, v8_scales, vs_words, vs_scales, b, out):
@@ -41,12 +41,14 @@ def tile_mix_fm_silu_kernel(tc, x, v8_words, v8_scales, vs_words, vs_scales, b, 
         psum = ctx.enter_context(tc.psum_pool(name="psum", bufs=BANKS_PER_SUM))
         ctx.enter_context(tc.manual_schedule())
 
-        v8_w = [keep.tile([P, PASSES, 4 * P], U8, name="v8_w%d" % m, align_bytes=64) for m in range(F_TILES)]
-        vs_w = [keep.tile([P, PASSES, 2 * P], U8, name="vs_w%d" % m, align_bytes=64) for m in range(F_TILES)]
+        halves = range(F_TILES // TILES_PER_LOAD)
+        half_f = TILES_PER_LOAD * P
+        v8_w = [keep.tile([P, PASSES, 4 * half_f], U8, name="v8_w%d" % half, align_bytes=64) for half in halves]
+        vs_w = [keep.tile([P, PASSES, 2 * half_f], U8, name="vs_w%d" % half, align_bytes=64) for half in halves]
         v8_plane = keep.tile([P, PASSES, F], U8, align_bytes=64)
         vs_plane = keep.tile([P, PASSES, F], U8, align_bytes=64)
         bias = keep.tile([P, QUADRANT], F32, align_bytes=64)
-        table_warm = keep.tile([P, 2], F32)
+        zeros = keep.tile([P, QUADRANT], F32)
         bias_rows = keep.tile([P, QUADRANT], F32, align_bytes=64)
 
         raw, rounded, codes, planes, banks, a_squared, diffs = {}, {}, {}, {}, {}, {}, {}
@@ -62,11 +64,14 @@ def tile_mix_fm_silu_kernel(tc, x, v8_words, v8_scales, vs_words, vs_scales, b, 
                 live = plane[QUADRANT * q : QUADRANT * q + 4, :, :]
                 queue.dma_start(out=live.bitcast(I32), in_=rows.bitcast(I32))
 
-        def load_weights(m):
-            v8_rows = v8_words.rearrange("a p f i -> p a (f i)").bitcast(I32)
-            vs_rows = vs_words.rearrange("a p n -> p a n").bitcast(I32)
-            nc.sync.dma_start(out=v8_w[m][:].bitcast(I32), in_=v8_rows[:, :, m * P : (m + 1) * P])
-            nc.sync.dma_start(out=vs_w[m][:].bitcast(I32), in_=vs_rows[:, :, m * P // 2 : (m + 1) * P // 2])
+        def load_v8(half):
+            rows = v8_words.rearrange("a p f i -> p a (f i)").bitcast(I32)
+            nc.sync.dma_start(out=v8_w[half][:].bitcast(I32), in_=rows[:, :, half * half_f : (half + 1) * half_f])
+
+        def load_vs(half):
+            rows = vs_words.rearrange("a p n -> p a n").bitcast(I32)
+            words = half_f // 2
+            nc.sync.dma_start(out=vs_w[half][:].bitcast(I32), in_=rows[:, :, half * words : (half + 1) * words])
 
         def load_bias():
             for q in range(QUADRANTS):
@@ -114,10 +119,13 @@ def tile_mix_fm_silu_kernel(tc, x, v8_words, v8_scales, vs_words, vs_scales, b, 
                     banks[c, h, operand] = psum.tile([P, BANK], F32, name="acc_" + operand)
                 steps = [(m, t0) for m in tiles_of(c, h) for t0 in range(0, width, n)]
                 for s, (m, t0) in enumerate(steps):
+                    half, place = divmod(m, TILES_PER_LOAD)
                     if operand == "x":
-                        weights, weight_plane = v8_w[m][:, g, :].bitcast(FP8X4), v8_plane
+                        weights = v8_w[half][:, g, 4 * P * place : 4 * P * (place + 1)].bitcast(FP8X4)
+                        weight_plane = v8_plane
                     else:
-                        weights, weight_plane = vs_w[m][:, g, :].bitcast(FP4X4), vs_plane
+                        weights = vs_w[half][:, g, 2 * P * place : 2 * P * (place + 1)].bitcast(FP4X4)
+                        weight_plane = vs_plane
                     nc.tensor.matmul_mx(
                         out=banks[c, h, operand][:, s * n : (s + 1) * n],
                         lhsT=weights,
@@ -165,46 +173,37 @@ def tile_mix_fm_silu_kernel(tc, x, v8_words, v8_scales, vs_words, vs_scales, b, 
             queue.dma_start(out=rows.rearrange("(m p) w -> p m w", p=P), in_=result[:])
 
         nc.vector.memset(v8_plane[:].bitcast(U32), 0)
-        nc.vector.memset(table_warm[:], 0.0)
+        nc.vector.memset(zeros[:], 0.0)
         nc.vector.memset(vs_plane[:].bitcast(U32), 0)
-        nc.vector.memset(bias_rows[:], 0.0)
 
         load_x(0, 0)
         load_scales(nc.scalar, v8_plane, v8_scales)
         load_scales(nc.gpsimd, vs_plane, vs_scales)
+        nc.scalar.activation(out=bias_rows[:], in_=zeros[:], func=ACT.Silu)
         load_x(0, 1)
-        load_weights(0)
+        load_v8(0)
         load_x(1, 0)
+        load_vs(0)
         load_bias()
-        load_weights(1)
         load_x(1, 1)
-        load_weights(2)
-        load_weights(3)
+        load_v8(1)
+        load_vs(1)
         load_x(2, 0)
         load_x(2, 1)
-
-        nc.scalar.activation(out=table_warm[:, 1:2], in_=table_warm[:, 0:1], func=ACT.Silu)
 
         round_x(0, 0)
         square_x(0, 0)
         quantize(0, 0, "x")
-        warm_bank = psum.tile([P, BANK], F32, name="acc_xs")
-        for n in range(WARM_PASSES):
-            nc.tensor.matmul_mx(
-                out=warm_bank[:],
-                lhsT=codes[0, 0, "x"][:, :P].bitcast(FP8X4),
-                lhsT_scale=planes[0, 0, "x"][:, :P],
-                rhs=codes[0, 0, "x"][:].bitcast(FP8X4),
-                rhs_scale=planes[0, 0, "x"][:],
-                start=True,
-                stop=True,
-            )
         round_x(0, 1)
         square_x(0, 1)
         quantize(0, 0, "xs")
         quantize(0, 1, "x")
         quantize(0, 1, "xs")
-        for h in range(GROUPS[0]):
+        multiply(0, 0, "x", range(TILES_PER_LOAD))
+        for h in range(TILES_PER_LOAD):
+            multiply(0, 1, "x", [h])
+            multiply_all_passes(0, "xs", h)
+        for h in range(TILES_PER_LOAD, GROUPS[0]):
             multiply_all_passes(0, "x", h)
             multiply_all_passes(0, "xs", h)
 

from contextlib import ExitStack

import concourse.mybir as mybir

K, F, T = 1024, 512, 1024
FLOPS = 2 * 2 * K * F * T

F32 = mybir.dt.float32
BF16 = mybir.dt.bfloat16
I32 = mybir.dt.int32
U32 = mybir.dt.uint32
U8 = mybir.dt.uint8
FP8X4 = mybir.dt.float8_e4m3fn_x4
FP4X4 = mybir.dt.float4_e2m1fn_x4
ACT = mybir.ActivationFunctionType
ALU = mybir.AluOpType

P = 128
QUADRANT = 32
QUADRANTS = P // QUADRANT
PACK = 4
K_PASS = P * PACK
PASSES = K // K_PASS
F_TILES = F // P
BANK = 512
BANKS_PER_SUM = 4
RUN = 4
N_FP4 = 128
WIDTHS = (512, 256, 256)
GROUPS = (4, 2, 4)
VECTOR_COLUMNS = (0, 64, 64)
TILES_PER_LOAD = 2


def tile_mix_fm_silu_kernel(tc, x, v8_words, v8_scales, vs_words, vs_scales, b, out):
    nc = tc.nc
    starts = [sum(WIDTHS[:c]) for c in range(len(WIDTHS))]

    with ExitStack() as ctx:
        keep = ctx.enter_context(tc.tile_pool(name="keep", bufs=1))
        psum = ctx.enter_context(tc.psum_pool(name="psum", bufs=BANKS_PER_SUM))
        ctx.enter_context(tc.manual_schedule())

        halves = range(F_TILES // TILES_PER_LOAD)
        half_f = TILES_PER_LOAD * P
        v8_w = [keep.tile([P, PASSES, 4 * half_f], U8, name="v8_w%d" % half, align_bytes=64) for half in halves]
        vs_w = [keep.tile([P, PASSES, 2 * half_f], U8, name="vs_w%d" % half, align_bytes=64) for half in halves]
        v8_plane = keep.tile([P, PASSES, F], U8, align_bytes=64)
        vs_plane = keep.tile([P, PASSES, F], U8, align_bytes=64)
        bias = keep.tile([P, QUADRANT], F32, align_bytes=64)
        zeros = keep.tile([P, QUADRANT], F32)
        bias_rows = keep.tile([P, QUADRANT], F32, align_bytes=64)

        raw, rounded, codes, planes, banks, a_squared, diffs = {}, {}, {}, {}, {}, {}, {}

        def load_x(c, g):
            raw[c, g] = keep.tile([P, PACK, WIDTHS[c]], F32, name="raw%d_%d" % (c, g))
            rows = x[g * K_PASS : (g + 1) * K_PASS, starts[c] : starts[c] + WIDTHS[c]]
            nc.sync.dma_start(out=raw[c, g][:], in_=rows.rearrange("(p j) w -> p j w", j=PACK))

        def load_scales(queue, plane, scales):
            for q in range(QUADRANTS):
                rows = scales[:, 4 * q : 4 * q + 4, :].rearrange("a r f -> r a f")
                live = plane[QUADRANT * q : QUADRANT * q + 4, :, :]
                queue.dma_start(out=live.bitcast(I32), in_=rows.bitcast(I32))

        def load_v8(half):
            rows = v8_words.rearrange("a p f i -> p a (f i)").bitcast(I32)
            nc.sync.dma_start(out=v8_w[half][:].bitcast(I32), in_=rows[:, :, half * half_f : (half + 1) * half_f])

        def load_vs(half):
            rows = vs_words.rearrange("a p n -> p a n").bitcast(I32)
            words = half_f // 2
            nc.sync.dma_start(out=vs_w[half][:].bitcast(I32), in_=rows[:, :, half * words : (half + 1) * words])

        def load_bias():
            for q in range(QUADRANTS):
                rows = b.rearrange("(m q i) -> q m i", q=QUADRANTS, i=QUADRANT)[q]
                nc.sync.dma_start(out=bias_rows[QUADRANT * q : QUADRANT * q + F_TILES, :], in_=rows)

        def interleaving_views(c, g, operand):
            rounded[c, g, operand] = keep.tile(
                [P, WIDTHS[c] * PACK], BF16, name="%s%d_%d" % (operand, c, g), align_bytes=64
            )
            dst = rounded[c, g, operand][:].rearrange("p (u i j) -> p u j i", i=RUN, j=PACK)
            src = raw[c, g][:].rearrange("p j (u i) -> p u j i", i=RUN)
            return dst, src

        def round_x(c, g):
            dst, src = interleaving_views(c, g, "x")
            nc.vector.tensor_copy(out=dst, in_=src)

        def square_x(c, g):
            dst, src = interleaving_views(c, g, "xs")
            cut = VECTOR_COLUMNS[c] // RUN
            if cut > 0:
                nc.vector.tensor_tensor(out=dst[:, :cut], in0=src[:, :cut], in1=src[:, :cut], op=ALU.mult)
            nc.scalar.activation(out=dst[:, cut:], in_=src[:, cut:], func=ACT.Square)

        def quantize(c, g, operand):
            key = (c, g, operand)
            codes[key] = keep.tile([P, WIDTHS[c]], U32, name="codes_%s%d_%d" % (operand, c, g), align_bytes=64)
            planes[key] = keep.tile([P, WIDTHS[c]], U8, name="plane_%s%d_%d" % (operand, c, g), align_bytes=64)
            nc.vector.quantize_mx(out=codes[key][:].bitcast(FP8X4), scales=planes[key][:], in_=rounded[key][:])

        def tiles_of(c, h):
            per_group = F_TILES // GROUPS[c]
            return range(h * per_group, (h + 1) * per_group)

        def span(c):
            return F_TILES // GROUPS[c] * WIDTHS[c]

        def multiply(c, g, operand, groups):
            key = (c, g, operand)
            width = WIDTHS[c]
            n = width if (operand == "x" or width == BANK) else N_FP4
            for h in groups:
                if g == 0:
                    banks[c, h, operand] = psum.tile([P, BANK], F32, name="acc_" + operand)
                steps = [(m, t0) for m in tiles_of(c, h) for t0 in range(0, width, n)]
                for s, (m, t0) in enumerate(steps):
                    half, place = divmod(m, TILES_PER_LOAD)
                    if operand == "x":
                        weights = v8_w[half][:, g, 4 * P * place : 4 * P * (place + 1)].bitcast(FP8X4)
                        weight_plane = v8_plane
                    else:
                        weights = vs_w[half][:, g, 2 * P * place : 2 * P * (place + 1)].bitcast(FP4X4)
                        weight_plane = vs_plane
                    nc.tensor.matmul_mx(
                        out=banks[c, h, operand][:, s * n : (s + 1) * n],
                        lhsT=weights,
                        lhsT_scale=weight_plane[:, g, P * m : P * (m + 1)],
                        rhs=codes[key][:, t0 : t0 + n].bitcast(FP8X4),
                        rhs_scale=planes[key][:, t0 : t0 + n],
                        start=(g == 0 and s == 0),
                        stop=(g == PASSES - 1 and s == len(steps) - 1),
                    )

        def multiply_all_passes(c, operand, h):
            for g in range(PASSES):
                multiply(c, g, operand, [h])

        def square_a(c, h):
            a_squared[c, h] = keep.tile([P, span(c)], F32, name="asq%d_%d" % (c, h))
            nc.scalar.activation(out=a_squared[c, h][:], in_=banks[c, h, "x"][:, : span(c)], func=ACT.Square)

        def square_a_on_vector(c, h):
            acc = banks[c, h, "x"][:, : span(c)]
            a_squared[c, h] = keep.tile([P, span(c)], F32, name="asq%d_%d" % (c, h))
            a_copy = keep.tile([P, span(c)], F32)
            nc.vector.tensor_copy(out=a_copy[:], in_=acc)
            nc.vector.tensor_tensor(out=a_squared[c, h][:], in0=a_copy[:], in1=acc, op=ALU.mult)

        def subtract(c, h):
            diffs[c, h] = keep.tile([P, span(c)], F32, name="diff%d_%d" % (c, h))
            nc.vector.tensor_tensor(
                out=diffs[c, h][:], in0=a_squared[c, h][:], in1=banks[c, h, "xs"][:, : span(c)], op=ALU.subtract
            )

        def finish(c, h, queue):
            width = WIDTHS[c]
            tiles = tiles_of(c, h)
            result = keep.tile([P, len(tiles), width], F32, name="res%d_%d" % (c, h))
            for s, m in enumerate(tiles):
                nc.scalar.activation(
                    out=result[:, s, :],
                    in_=diffs[c, h][:, s * width : (s + 1) * width],
                    func=ACT.Silu,
                    bias=bias[:, m : m + 1],
                    scale=0.5,
                )
            rows = out[tiles[0] * P : (tiles[-1] + 1) * P, starts[c] : starts[c] + width]
            queue.dma_start(out=rows.rearrange("(m p) w -> p m w", p=P), in_=result[:])

        nc.vector.memset(v8_plane[:].bitcast(U32), 0)
        nc.vector.memset(zeros[:], 0.0)
        nc.vector.memset(vs_plane[:].bitcast(U32), 0)

        load_x(0, 0)
        load_scales(nc.scalar, v8_plane, v8_scales)
        load_scales(nc.gpsimd, vs_plane, vs_scales)
        nc.scalar.activation(out=bias_rows[:], in_=zeros[:], func=ACT.Silu)
        load_x(0, 1)
        load_v8(0)
        load_x(1, 0)
        load_vs(0)
        load_bias()
        load_x(1, 1)
        load_v8(1)
        load_vs(1)
        load_x(2, 0)
        load_x(2, 1)

        round_x(0, 0)
        square_x(0, 0)
        quantize(0, 0, "x")
        round_x(0, 1)
        square_x(0, 1)
        quantize(0, 0, "xs")
        quantize(0, 1, "x")
        quantize(0, 1, "xs")
        multiply(0, 0, "x", range(TILES_PER_LOAD))
        for h in range(TILES_PER_LOAD):
            multiply(0, 1, "x", [h])
            multiply_all_passes(0, "xs", h)
        for h in range(TILES_PER_LOAD, GROUPS[0]):
            multiply_all_passes(0, "x", h)
            multiply_all_passes(0, "xs", h)

        round_x(1, 0)
        square_x(1, 0)
        square_a(0, 0)
        quantize(1, 0, "x")
        subtract(0, 0)
        square_a(0, 1)
        nc.vector.transpose(out=bias[:], in_=bias_rows[:])

        round_x(1, 1)
        square_x(1, 1)
        finish(0, 0, nc.sync)
        quantize(1, 0, "xs")
        subtract(0, 1)
        square_a(0, 2)
        quantize(1, 1, "x")
        quantize(1, 1, "xs")
        finish(0, 1, nc.sync)
        for operand in ("x", "xs"):
            for h in range(GROUPS[1]):
                multiply_all_passes(1, operand, h)
        subtract(0, 2)
        square_a(0, 3)

        round_x(2, 0)
        square_x(2, 0)
        finish(0, 2, nc.sync)
        quantize(2, 0, "x")
        multiply(2, 0, "x", [0, 1])
        subtract(0, 3)

        round_x(2, 1)
        square_a(1, 0)
        square_x(2, 1)
        square_a(1, 1)
        quantize(2, 0, "xs")
        multiply(2, 0, "xs", [0, 1])
        quantize(2, 1, "x")
        multiply(2, 0, "x", [2, 3])
        multiply(2, 1, "x", [0, 1])
        finish(0, 3, nc.sync)
        subtract(1, 0)
        multiply(2, 0, "xs", [2])
        multiply(2, 1, "x", [2, 3])
        quantize(2, 1, "xs")
        multiply(2, 1, "xs", [0, 1, 2])
        subtract(1, 1)
        multiply_all_passes(2, "xs", 3)

        last = GROUPS[2] - 1
        finish(1, 0, nc.sync)
        square_a(2, 0)
        finish(1, 1, nc.sync)
        for h in range(1, last):
            square_a(2, h)
        square_a_on_vector(2, last)
        for h in range(GROUPS[2]):
            subtract(2, h)
            finish(2, h, nc.scalar if h == last else nc.sync)
